import numpy as np
import ml_dtypes


def mxq(x, axis, fmt="e4m3"):
    dtype, down = {"e4m3": (ml_dtypes.float8_e4m3fn, 7), "e5m2": (ml_dtypes.float8_e5m2, 14)}[fmt]
    v = np.moveaxis(np.asarray(x, np.float32).astype(ml_dtypes.bfloat16).astype(np.float64), axis, -1)
    blocks = v.reshape(v.shape[:-1] + (-1, 32))
    amax = np.abs(blocks).max(-1, keepdims=True)
    byte = np.maximum(np.where(amax > 0, np.frexp(amax)[1] - 1 + 127, 0) - down, 1)
    scale = np.exp2(byte - 127.0)
    codes = (blocks / scale).astype(np.float32).astype(dtype).astype(np.float64)
    return np.moveaxis((codes * scale).reshape(v.shape), -1, axis)


WIDE = False


def mx_kscale(k):
    if not WIDE:
        return np.ones(k)
    levels = np.array([10, -10, 5, -5, 0])
    if k % 512:
        return np.exp2(np.random.permutation(np.resize(levels, k // 32))).repeat(32)
    a = np.empty((k // 512, 16))
    for p in range(k // 512):
        a[p, :8] = np.random.permutation(np.resize(levels, 8))
        for g in range(8):
            far = levels[np.abs(levels - a[p, g]) >= 10]
            a[p, g + 8] = far[np.random.randint(len(far))]
    return np.exp2(a.ravel()).repeat(32)


def f64(x):
    return np.asarray(x).astype(np.float64)


def striped(idx):
    return np.tile(np.asarray(idx).reshape(-1, 16).T, (8, 1)).astype(np.uint16)


def unstriped(offs):
    return offs[:16].T.reshape(-1).astype(np.int64)


E2M1 = np.array([0.0, 0.5, 1.0, 1.5, 2.0, 3.0, 4.0, 6.0, -0.0, -0.5, -1.0, -1.5, -2.0, -3.0, -4.0, -6.0])


def pack_weight(w, fmt):
    k, n = w.shape
    w = f64(np.asarray(w, np.float32).astype(ml_dtypes.bfloat16)).reshape(k // 32, 32, n)
    amax = np.abs(w).max(1)
    if fmt == "e4m3":
        byte = np.frexp(amax)[1] - 1 + 127 - 7
    else:
        mant, ex = np.frexp(amax / 6.0)
        byte = np.where(mant > 0.5, ex, ex - 1) + 127
    byte = np.clip(np.where(amax > 0, byte, 1), 1, 254)
    scaled = (w * np.exp2(127.0 - byte)[:, None, :]).reshape(k, n).astype(np.float32)
    by_word = np.ascontiguousarray(scaled.reshape(k // 512, 128, 4, n).transpose(0, 1, 3, 2))
    if fmt == "e4m3":
        words = by_word.astype(ml_dtypes.float8_e4m3fn).view(np.uint8)
    else:
        c = by_word.astype(ml_dtypes.float4_e2m1fn).view(np.uint8) & 0xF
        words = (c[..., 0::2] | (c[..., 1::2] << 4)).reshape(k // 512, 128, 2 * n)
    return np.ascontiguousarray(words), np.ascontiguousarray(byte.astype(np.uint8).reshape(k // 512, 16, n))


def unpack_weight(words, scales, fmt):
    g, _, n = scales.shape
    words = np.ascontiguousarray(words).reshape(g, 128, n, -1)
    if fmt == "e4m3":
        vals = words.view(ml_dtypes.float8_e4m3fn).astype(np.float64)
    else:
        nib = np.empty((g, 128, n, 4), np.uint8)
        nib[..., 0::2] = words & 0xF
        nib[..., 1::2] = words >> 4
        vals = E2M1[nib]
    vals = vals * np.repeat(np.exp2(scales.astype(np.float64) - 127.0), 8, axis=1)[..., None]
    return vals.transpose(0, 1, 3, 2).reshape(g * 512, n)


def bf(x):
    return np.asarray(x, np.float32).astype(ml_dtypes.bfloat16)


def planes(Y):
    r, m = Y.shape
    b = f64(bf(Y)).reshape(r // 32, 32, m)
    amax = np.abs(b).max(1)
    byte = np.clip(np.where(amax > 0, np.frexp(amax)[1] - 1 + 127 - 7, 1), 1, 254)
    codes = (b * np.exp2(127.0 - byte)[:, None, :]).reshape(r, m).astype(np.float32).astype(ml_dtypes.float8_e4m3fn).view(np.uint8)
    words = codes.reshape(r // 512, 128, 4, m).transpose(0, 1, 3, 2)
    return np.ascontiguousarray(words), np.ascontiguousarray(byte.astype(np.uint8).reshape(r // 512, 16, m))


K, T, J, I, N, R = 1024, 1024, 512, 512, 512, 512


def setup_inputs():
    n = np.random.standard_normal
    idx = np.random.permutation(T)[:J]
    idx2 = np.random.permutation(T)[:I]
    fk = mx_kscale(K)
    fr = mx_kscale(R)
    xqp = pack_weight(n((K, T)) / fk[:, None], "e2m1")
    lowp = pack_weight(n((K, R)) * 1 / np.sqrt(K) * fk[:, None] * fr, "e4m3")
    upp = pack_weight(n((R, N)) * 1 / np.sqrt(R) / fr[:, None], "e2m1")
    return {
        "xq_words": xqp[0],
        "xq_scales": xqp[1],
        "wa": (n((K, N)) * 1 / np.sqrt(K) * fk[:, None]).astype(np.float32),
        "low_words": lowp[0],
        "low_scales": lowp[1],
        "up_words": upp[0],
        "up_scales": upp[1],
        "ga": (np.random.uniform(0.4, 1.2, (1, J))).astype(np.float32),
        "offs": striped(idx),
        "offs2": striped(idx2),
    }


def reference(xq_words, xq_scales, wa, low_words, low_scales, up_words, up_scales, ga, offs, offs2):
    idx = unstriped(offs)
    idx2 = unstriped(offs2)
    xqu = unpack_weight(xq_words, xq_scales, "e2m1")
    lowu = unpack_weight(low_words, low_scales, "e4m3")
    upu = unpack_weight(up_words, up_scales, "e2m1")
    waq = mxq(f64(wa), 0, "e4m3")
    xqidxg = xqu[:, idx]
    p = waq.T @ xqidxg
    xqidx2g = xqu[:, idx2]
    u = lowu.T @ xqidx2g
    v = np.abs(u) - 0.5 * u
    vq = mxq(v, 0, "e4m3")
    q = upu.T @ vq
    pw = p * f64(ga)
    pg = np.zeros((N, T))
    pg[:, idx] = pw
    qg = np.zeros((N, T))
    qg[:, idx2] = q
    y = pg + qg
    words, scales = planes(y)
    return y, words, scales

@@ -1,0 +1,199 @@
+from contextlib import ExitStack
+
+import concourse.mybir as mybir
+
+K, T, J, N, R = 1024, 1024, 512, 512, 512
+FLOPS = 2 * K * N * J + 2 * K * R * J + 2 * R * N * J
+
+F32 = mybir.dt.float32
+BF16 = mybir.dt.bfloat16
+I32 = mybir.dt.int32
+U32 = mybir.dt.uint32
+U16 = mybir.dt.uint16
+U8 = mybir.dt.uint8
+FP8X4 = mybir.dt.float8_e4m3fn_x4
+FP4X4 = mybir.dt.float4_e2m1fn_x4
+ALU = mybir.AluOpType
+ACT = mybir.ActivationFunctionType
+
+P = 128
+PACK = 4
+QUADS = 4
+PASSES = K // (P * PACK)
+
+
+def tile_list_two_roads_one_layer_pl_kernel(tc, xq_words, xq_scales, wa, low_words, low_scales, up_words, up_scales, ga, offs, offs2, out_0, out_1, out_2):
+    nc = tc.nc
+    with ExitStack() as ctx:
+        keep = ctx.enter_context(tc.tile_pool(name="keep", bufs=1))
+        psum = ctx.enter_context(tc.psum_pool(name="psum", bufs=1))
+
+        def tile(shape, dtype, name):
+            return keep.tile(shape, dtype, name=name, align_bytes=64)
+
+        list1 = keep.tile([P, J // 16], U16, name="list1")
+        list2 = keep.tile([P, J // 16], U16, name="list2")
+        x_words = [tile([P, T], U16, f"x_words{z}") for z in range(PASSES)]
+        x_scales = tile([P, T], U8, "x_scales")
+        low_raw = tile([P, PASSES, R], I32, "low_raw")
+        low_scale_raw = tile([P, PASSES, R], U8, "low_scale_raw")
+        up_raw = tile([P, N], U16, "up_raw")
+        up_scale_raw = tile([P, N], U8, "up_scale_raw")
+        wa_raw = [tile([P, PACK, N], F32, f"wa_raw{z}") for z in range(PASSES)]
+        gate = tile([P, J], F32, "gate")
+        shifted = [tile([P, J], U8, f"shifted{a}") for a in range(2)]
+
+        p_pages = [tile([P, T], F32, f"p_page{a}") for a in range(2)]
+        q_pages = [tile([P, T], F32, f"q_page{a}") for a in range(2)]
+        nc.vector.memset(x_scales[:].bitcast(I32), 0)
+        nc.gpsimd.memset(low_scale_raw[:].rearrange("p z c -> p (z c)").bitcast(I32), 0)
+        for a in range(2):
+            nc.gpsimd.memset(shifted[1 - a][:].bitcast(I32), 0)
+        nc.gpsimd.memset(up_scale_raw[:].bitcast(I32), 0)
+        for a in range(2):
+            nc.vector.memset(q_pages[a][:], 0.0)
+            nc.gpsimd.memset(p_pages[a][:], 0.0)
+
+        wa_rows = wa.rearrange("(z p j) n -> z p j n", z=PASSES, j=PACK)
+        nc.sync.dma_start(list2[:], offs2)
+        for z in range(PASSES):
+            nc.sync.dma_start(out=x_words[z][:].bitcast(I32), in_=xq_words[z].bitcast(I32))
+        for q in range(QUADS):
+            nc.sync.dma_start(out=x_scales[32 * q : 32 * q + 8, :].bitcast(I32), in_=xq_scales[:, 4 * q : 4 * q + 4, :].bitcast(I32))
+        nc.sync.dma_start(out=wa_raw[0][:], in_=wa_rows[0])
+        nc.sync.dma_start(out=low_raw[:], in_=low_words.rearrange("z p c r -> p z (c r)").bitcast(I32))
+        nc.sync.dma_start(out=wa_raw[1][:], in_=wa_rows[1])
+        nc.sync.dma_start(list1[:], offs)
+        for q in range(QUADS):
+            nc.sync.dma_start(out=low_scale_raw[32 * q : 32 * q + 4, :, :].bitcast(I32), in_=low_scales[:, 4 * q : 4 * q + 4, :].rearrange("z r c -> r z c").bitcast(I32))
+
+        def gather(offsets, a):
+            scales = tile([P, J], U8, f"picked_scales{a}")
+            nc.vector.tensor_copy(out=scales[:], in_=x_scales[:].indirect(offsets[:]))
+            nc.sync.dma_start(out=shifted[a][0:100, :].bitcast(I32), in_=scales[4:104, :].bitcast(I32))
+            words = []
+            for z in range(PASSES):
+                picked = tile([P, J], U16, f"picked_words{a}{z}")
+                nc.vector.tensor_copy(out=picked[:], in_=x_words[z][:].indirect(offsets[:]))
+                words.append(picked)
+            return words, [scales, shifted[a]]
+
+        words2, scales2 = gather(list2, 1)
+
+        nc.sync.dma_start(out=up_raw[:].bitcast(I32), in_=up_words[0].bitcast(I32))
+        for q in range(QUADS):
+            nc.sync.dma_start(out=up_scale_raw[32 * q : 32 * q + 4, :].bitcast(I32), in_=up_scales[0, 4 * q : 4 * q + 4, :].bitcast(I32))
+        nc.sync.dma_start(out=gate[:], in_=ga[0].partition_broadcast(P))
+
+        low_codes = tile([P, PASSES, R], I32, "low_codes")
+        low_scale = tile([P, PASSES, R], U8, "low_scale")
+        for z in range(PASSES):
+            nc.gpsimd.tensor_copy(out=low_codes[:, z, :].rearrange("p (t m) -> p t m", t=PACK), in_=low_raw[:, z, :].rearrange("p (m t) -> p t m", t=PACK))
+            nc.gpsimd.tensor_copy(out=low_scale[:, z, :].rearrange("p (t m) -> p t m", t=PACK), in_=low_scale_raw[:, z, :].rearrange("p (m t) -> p t m", t=PACK))
+        up_codes = tile([P, 2 * N], U8, "up_codes")
+        up_scale = tile([P, N], U8, "up_scale")
+        nc.gpsimd.tensor_copy(out=up_codes[:].rearrange("p (t m b) -> p t m b", t=PACK, b=2), in_=up_raw[:].bitcast(U8).rearrange("p (m t b) -> p t m b", t=PACK, b=2))
+        nc.gpsimd.tensor_copy(out=up_scale[:].rearrange("p (t m) -> p t m", t=PACK), in_=up_scale_raw[:].rearrange("p (m t) -> p t m", t=PACK))
+
+        words1, scales1 = gather(list1, 0)
+
+        v_bf = tile([P, J * PACK], BF16, "v_bf")
+        v_codes = tile([P, J], U32, "v_codes")
+        v_scale = tile([P, J], U8, "v_scale")
+        for c in range(J // P):
+            cols = slice(c * P, (c + 1) * P)
+            u = psum.tile([P, PACK, P], F32, name="u", tag=f"second{c}")
+            for t in range(PACK):
+                for z in range(PASSES):
+                    nc.tensor.matmul_mx(
+                        out=u[:, t, :],
+                        lhsT=low_codes[:, z, t * P : (t + 1) * P].bitcast(FP8X4),
+                        lhsT_scale=low_scale[:, z, t * P : (t + 1) * P],
+                        rhs=words2[z][:, cols].bitcast(FP4X4),
+                        rhs_scale=scales2[z][:, cols],
+                        start=(z == 0),
+                        stop=(z == PASSES - 1),
+                    )
+            size = tile([P, P, PACK], F32, f"size{c}")
+            nc.scalar.activation(out=size[:], in_=u[:].rearrange("p t i -> p i t"), func=ACT.Abs)
+            nc.vector.scalar_tensor_tensor(
+                out=v_bf[:, c * P * PACK : (c + 1) * P * PACK].rearrange("p (i t) -> p i t", t=PACK),
+                in0=u[:].rearrange("p t i -> p i t"),
+                scalar=-0.5,
+                in1=size[:],
+                op0=ALU.mult,
+                op1=ALU.add,
+            )
+        nc.vector.quantize_mx(out=v_codes[:].bitcast(FP8X4), scales=v_scale[:], in_=v_bf[:])
+
+        wa_codes = tile([P, PASSES, N], U32, "wa_codes")
+        wa_scale = tile([P, PASSES, N], U8, "wa_scale")
+        for z in range(PASSES):
+            wa_bf = tile([P, N * PACK], BF16, f"wa_bf{z}")
+            dealt = wa_bf[:].rearrange("p (t h m j) -> p h m j t", t=PACK, h=2, j=PACK)
+            for h in range(2):
+                nc.scalar.copy(out=dealt[:, h], in_=wa_raw[z][:].rearrange("p j (h m t) -> p h m j t", h=2, t=PACK)[:, h])
+            nc.vector.quantize_mx(out=wa_codes[:, z, :].bitcast(FP8X4), scales=wa_scale[:, z, :], in_=wa_bf[:])
+
+        y = tile([P, PACK, T], F32, "y")
+        out_rows = out_0.rearrange("(p t) c -> p t c", t=PACK)
+        half = J // 2
+        for t in range(PACK):
+            rows = slice(t * P, (t + 1) * P)
+            q_sum = psum.tile([P, J], F32, name="q_sum", tag=f"second{t}")
+            nc.tensor.matmul_mx(
+                out=q_sum[:],
+                lhsT=up_codes[:, 2 * t * P : 2 * (t + 1) * P].bitcast(FP4X4),
+                lhsT_scale=up_scale[:, rows],
+                rhs=v_codes[:].bitcast(FP8X4),
+                rhs_scale=v_scale[:],
+                start=True,
+                stop=True,
+            )
+            p_sum = psum.tile([P, J], F32, name="p_sum", tag=f"first{t}")
+            for z in range(PASSES):
+                nc.tensor.matmul_mx(
+                    out=p_sum[:],
+                    lhsT=wa_codes[:, z, rows].bitcast(FP8X4),
+                    lhsT_scale=wa_scale[:, z, rows],
+                    rhs=words1[z][:].bitcast(FP4X4),
+                    rhs_scale=scales1[z][:],
+                    start=(z == 0),
+                    stop=(z == PASSES - 1),
+                )
+            q_vals = tile([P, J], F32, f"q_vals{t}")
+            nc.scalar.copy(out=q_vals[:], in_=q_sum[:])
+            q_page = q_pages[t % len(q_pages)]
+            for h in range(2):
+                nc.scalar.activation(out=q_page[:].indirect(list2[:, 16 * h : 16 * (h + 1)]), in_=q_vals[:, h * half : (h + 1) * half], func=ACT.Copy)
+            pw = tile([P, J], F32, f"pw{t}")
+            nc.vector.tensor_tensor(out=pw[:], in0=p_sum[:], in1=gate[:], op=ALU.mult)
+            p_page = p_pages[t % len(p_pages)]
+            if t < PACK - 1:
+                nc.vector.tensor_copy(out=p_page[:].indirect(list1[:]), in_=pw[:])
+            else:
+                nc.vector.tensor_copy(out=p_page[:].indirect(list1[:, 0:16]), in_=pw[:, 0:half])
+                nc.scalar.activation(out=p_page[:].indirect(list1[:, 16:32]), in_=pw[:, half:J], func=ACT.Copy)
+            adder = nc.gpsimd if t < PACK - 1 else nc.vector
+            adder.tensor_tensor(out=y[:, t, :], in0=p_page[:], in1=q_page[:], op=ALU.add)
+            nc.sync.dma_start(out=out_rows[:, t, :], in_=y[:, t, :])
+
+        y_codes = tile([P, T], U32, "y_codes")
+        y_scale = tile([P, T], U8, "y_scale")
+        words_out = out_1[0].rearrange("p c r -> p (c r)").bitcast(I32)
+        width = T // 4
+        for c in range(4):
+            cols = slice(c * width, (c + 1) * width)
+            y_bf = tile([P, width * PACK], BF16, f"y_bf{c}")
+            dst = y_bf[:].rearrange("p (c i t) -> p c t i", i=4, t=PACK)
+            src = y[:, :, cols].rearrange("p t (c i) -> p c t i", i=4)
+            if c % 2 == 0:
+                nc.vector.tensor_copy(out=dst, in_=src)
+            else:
+                nc.scalar.copy(out=dst, in_=src)
+            nc.vector.quantize_mx(out=y_codes[:, cols].bitcast(FP8X4), scales=y_scale[:, cols], in_=y_bf[:])
+            if c % 2 == 1:
+                both = slice((c - 1) * width, (c + 1) * width)
+                nc.sync.dma_start(out=words_out[:, both], in_=y_codes[:, both].bitcast(I32))
+        for q in range(QUADS):
+            nc.scalar.dma_start(out=out_2[0, 4 * q : 4 * q + 4, :].bitcast(I32), in_=y_scale[32 * q : 32 * q + 4, :].bitcast(I32))

@@ -28,54 +28,51 @@ def tile_list_two_roads_one_layer_pl_kernel(tc, xq_words, xq_scales, wa, low_wor
         keep = ctx.enter_context(tc.tile_pool(name="keep", bufs=1))
         psum = ctx.enter_context(tc.psum_pool(name="psum", bufs=1))
 
-        def tile(shape, dtype, name):
-            return keep.tile(shape, dtype, name=name, align_bytes=64)
+        def tile(shape, dtype, name, tag=None):
+            return keep.tile(shape, dtype, name=name, tag=tag or name, align_bytes=64)
 
         list1 = keep.tile([P, J // 16], U16, name="list1")
         list2 = keep.tile([P, J // 16], U16, name="list2")
         x_words = [tile([P, T], U16, f"x_words{z}") for z in range(PASSES)]
         x_scales = tile([P, T], U8, "x_scales")
-        low_raw = tile([P, PASSES, R], I32, "low_raw")
+        low_raw = tile([P, PASSES, R], U32, "low_raw")
         low_scale_raw = tile([P, PASSES, R], U8, "low_scale_raw")
         up_raw = tile([P, N], U16, "up_raw")
         up_scale_raw = tile([P, N], U8, "up_scale_raw")
         wa_raw = [tile([P, PACK, N], F32, f"wa_raw{z}") for z in range(PASSES)]
         gate = tile([P, J], F32, "gate")
         shifted = [tile([P, J], U8, f"shifted{a}") for a in range(2)]
-
         p_pages = [tile([P, T], F32, f"p_page{a}") for a in range(2)]
         q_pages = [tile([P, T], F32, f"q_page{a}") for a in range(2)]
-        nc.vector.memset(x_scales[:].bitcast(I32), 0)
+
+        nc.gpsimd.memset(x_scales[:].bitcast(I32), 0)
         nc.gpsimd.memset(low_scale_raw[:].rearrange("p z c -> p (z c)").bitcast(I32), 0)
         for a in range(2):
             nc.gpsimd.memset(shifted[1 - a][:].bitcast(I32), 0)
         nc.gpsimd.memset(up_scale_raw[:].bitcast(I32), 0)
-        for a in range(2):
-            nc.vector.memset(q_pages[a][:], 0.0)
-            nc.gpsimd.memset(p_pages[a][:], 0.0)
+        for page in q_pages + p_pages:
+            nc.vector.memset(page[:], 0.0)
 
         wa_rows = wa.rearrange("(z p j) n -> z p j n", z=PASSES, j=PACK)
         nc.sync.dma_start(list2[:], offs2)
-        for z in range(PASSES):
-            nc.sync.dma_start(out=x_words[z][:].bitcast(I32), in_=xq_words[z].bitcast(I32))
+        nc.sync.dma_start(out=x_words[0][:].bitcast(I32), in_=xq_words[0].bitcast(I32))
         for q in range(QUADS):
             nc.sync.dma_start(out=x_scales[32 * q : 32 * q + 8, :].bitcast(I32), in_=xq_scales[:, 4 * q : 4 * q + 4, :].bitcast(I32))
-        nc.sync.dma_start(out=wa_raw[0][:], in_=wa_rows[0])
-        nc.sync.dma_start(out=low_raw[:], in_=low_words.rearrange("z p c r -> p z (c r)").bitcast(I32))
-        nc.sync.dma_start(out=wa_raw[1][:], in_=wa_rows[1])
-        nc.sync.dma_start(list1[:], offs)
+        nc.sync.dma_start(out=x_words[1][:].bitcast(I32), in_=xq_words[1].bitcast(I32))
+        nc.sync.dma_start(out=low_raw[:].bitcast(I32), in_=low_words.rearrange("z p c r -> p z (c r)").bitcast(I32))
         for q in range(QUADS):
             nc.sync.dma_start(out=low_scale_raw[32 * q : 32 * q + 4, :, :].bitcast(I32), in_=low_scales[:, 4 * q : 4 * q + 4, :].rearrange("z r c -> r z c").bitcast(I32))
+        nc.sync.dma_start(list1[:], offs)
+        for z in range(PASSES):
+            nc.sync.dma_start(out=wa_raw[z][:], in_=wa_rows[z])
 
         def gather(offsets, a):
+            words = [tile([P, J], U16, f"picked_words{a}{z}") for z in range(PASSES)]
             scales = tile([P, J], U8, f"picked_scales{a}")
             nc.vector.tensor_copy(out=scales[:], in_=x_scales[:].indirect(offsets[:]))
             nc.sync.dma_start(out=shifted[a][0:100, :].bitcast(I32), in_=scales[4:104, :].bitcast(I32))
-            words = []
             for z in range(PASSES):
-                picked = tile([P, J], U16, f"picked_words{a}{z}")
-                nc.vector.tensor_copy(out=picked[:], in_=x_words[z][:].indirect(offsets[:]))
-                words.append(picked)
+                nc.vector.tensor_copy(out=words[z][:], in_=x_words[z][:].indirect(offsets[:]))
             return words, [scales, shifted[a]]
 
         words2, scales2 = gather(list2, 1)
@@ -85,17 +82,30 @@ def tile_list_two_roads_one_layer_pl_kernel(tc, xq_words, xq_scales, wa, low_wor
             nc.sync.dma_start(out=up_scale_raw[32 * q : 32 * q + 4, :].bitcast(I32), in_=up_scales[0, 4 * q : 4 * q + 4, :].bitcast(I32))
         nc.sync.dma_start(out=gate[:], in_=ga[0].partition_broadcast(P))
 
-        low_codes = tile([P, PASSES, R], I32, "low_codes")
+        low_codes = tile([P, PASSES, R], U32, "low_codes")
         low_scale = tile([P, PASSES, R], U8, "low_scale")
-        for z in range(PASSES):
-            nc.gpsimd.tensor_copy(out=low_codes[:, z, :].rearrange("p (t m) -> p t m", t=PACK), in_=low_raw[:, z, :].rearrange("p (m t) -> p t m", t=PACK))
-            nc.gpsimd.tensor_copy(out=low_scale[:, z, :].rearrange("p (t m) -> p t m", t=PACK), in_=low_scale_raw[:, z, :].rearrange("p (m t) -> p t m", t=PACK))
-        up_codes = tile([P, 2 * N], U8, "up_codes")
-        up_scale = tile([P, N], U8, "up_scale")
-        nc.gpsimd.tensor_copy(out=up_codes[:].rearrange("p (t m b) -> p t m b", t=PACK, b=2), in_=up_raw[:].bitcast(U8).rearrange("p (m t b) -> p t m b", t=PACK, b=2))
-        nc.gpsimd.tensor_copy(out=up_scale[:].rearrange("p (t m) -> p t m", t=PACK), in_=up_scale_raw[:].rearrange("p (m t) -> p t m", t=PACK))
+        nc.scalar.copy(out=low_codes[:].rearrange("p z (t m) -> p z m t", t=PACK), in_=low_raw[:].rearrange("p z (m t) -> p z m t", t=PACK))
+        nc.vector.tensor_copy(out=low_scale[:].rearrange("p z (t m) -> p z t m", t=PACK), in_=low_scale_raw[:].rearrange("p z (m t) -> p z t m", t=PACK))
 
         words1, scales1 = gather(list1, 0)
+
+        up_codes = tile([P, N], U16, "up_codes")
+        up_scale = tile([P, N], U8, "up_scale")
+        wa_bf, wa_codes, wa_scale = {}, {}, {}
+
+        def round_wa(z, h, copy, tag=None):
+            wa_bf[z, h] = tile([P, 2 * P * PACK], BF16, f"wa_bf{z}{h}", tag)
+            copy(out=wa_bf[z, h][:].rearrange("p (e m j) -> p m j e", e=2, j=PACK), in_=wa_raw[z][:].rearrange("p j (m h e) -> p h m j e", h=2, e=2)[:, h])
+
+        def quantise_wa(z, h, tag=None):
+            wa_codes[z, h] = tile([P, 2 * P], U32, f"wa_codes{z}{h}", tag)
+            wa_scale[z, h] = tile([P, 2 * P], U8, f"wa_scale{z}{h}")
+            nc.vector.quantize_mx(out=wa_codes[z, h][:].bitcast(FP8X4), scales=wa_scale[z, h][:], in_=wa_bf[z, h][:])
+
+        nc.scalar.copy(out=up_codes[:].rearrange("p (t m) -> p m t", t=PACK), in_=up_raw[:].rearrange("p (m t) -> p m t", t=PACK))
+        nc.vector.tensor_copy(out=up_scale[:].rearrange("p (t m) -> p t m", t=PACK), in_=up_scale_raw[:].rearrange("p (m t) -> p t m", t=PACK))
+        for h in range(2):
+            round_wa(0, h, nc.scalar.copy)
 
         v_bf = tile([P, J * PACK], BF16, "v_bf")
         v_codes = tile([P, J], U32, "v_codes")
@@ -124,16 +134,13 @@ def tile_list_two_roads_one_layer_pl_kernel(tc, xq_words, xq_scales, wa, low_wor
                 op0=ALU.mult,
                 op1=ALU.add,
             )
+        quantise_wa(0, 0, "size3")
         nc.vector.quantize_mx(out=v_codes[:].bitcast(FP8X4), scales=v_scale[:], in_=v_bf[:])
-
-        wa_codes = tile([P, PASSES, N], U32, "wa_codes")
-        wa_scale = tile([P, PASSES, N], U8, "wa_scale")
-        for z in range(PASSES):
-            wa_bf = tile([P, N * PACK], BF16, f"wa_bf{z}")
-            dealt = wa_bf[:].rearrange("p (t h m j) -> p h m j t", t=PACK, h=2, j=PACK)
-            for h in range(2):
-                nc.scalar.copy(out=dealt[:, h], in_=wa_raw[z][:].rearrange("p j (h m t) -> p h m j t", h=2, t=PACK)[:, h])
-            nc.vector.quantize_mx(out=wa_codes[:, z, :].bitcast(FP8X4), scales=wa_scale[:, z, :], in_=wa_bf[:])
+        round_wa(1, 0, nc.scalar.copy, "size1")
+        quantise_wa(1, 0)
+        round_wa(1, 1, nc.scalar.copy, "size2")
+        quantise_wa(0, 1, "v_bf")
+        quantise_wa(1, 1)
 
         y = tile([P, PACK, T], F32, "y")
         out_rows = out_0.rearrange("(p t) c -> p t c", t=PACK)
@@ -143,7 +150,7 @@ def tile_list_two_roads_one_layer_pl_kernel(tc, xq_words, xq_scales, wa, low_wor
             q_sum = psum.tile([P, J], F32, name="q_sum", tag=f"second{t}")
             nc.tensor.matmul_mx(
                 out=q_sum[:],
-                lhsT=up_codes[:, 2 * t * P : 2 * (t + 1) * P].bitcast(FP4X4),
+                lhsT=up_codes[:, rows].bitcast(FP4X4),
                 lhsT_scale=up_scale[:, rows],
                 rhs=v_codes[:].bitcast(FP8X4),
                 rhs_scale=v_scale[:],
@@ -154,46 +161,47 @@ def tile_list_two_roads_one_layer_pl_kernel(tc, xq_words, xq_scales, wa, low_wor
             for z in range(PASSES):
                 nc.tensor.matmul_mx(
                     out=p_sum[:],
-                    lhsT=wa_codes[:, z, rows].bitcast(FP8X4),
-                    lhsT_scale=wa_scale[:, z, rows],
+                    lhsT=wa_codes[z, t // 2][:, (t % 2) * P : (t % 2 + 1) * P].bitcast(FP8X4),
+                    lhsT_scale=wa_scale[z, t // 2][:, (t % 2) * P : (t % 2 + 1) * P],
                     rhs=words1[z][:].bitcast(FP4X4),
                     rhs_scale=scales1[z][:],
                     start=(z == 0),
                     stop=(z == PASSES - 1),
                 )
+            p_vals = tile([P, J], F32, f"p_vals{t}")
+            p_page = p_pages[t % len(p_pages)]
+            nc.vector.tensor_tensor(out=p_vals[:], in0=p_sum[:], in1=gate[:], op=ALU.mult)
+            nc.vector.tensor_copy(out=p_page[:].indirect(list1[:]), in_=p_vals[:])
             q_vals = tile([P, J], F32, f"q_vals{t}")
             nc.scalar.copy(out=q_vals[:], in_=q_sum[:])
             q_page = q_pages[t % len(q_pages)]
             for h in range(2):
                 nc.scalar.activation(out=q_page[:].indirect(list2[:, 16 * h : 16 * (h + 1)]), in_=q_vals[:, h * half : (h + 1) * half], func=ACT.Copy)
-            pw = tile([P, J], F32, f"pw{t}")
-            nc.vector.tensor_tensor(out=pw[:], in0=p_sum[:], in1=gate[:], op=ALU.mult)
-            p_page = p_pages[t % len(p_pages)]
-            if t < PACK - 1:
-                nc.vector.tensor_copy(out=p_page[:].indirect(list1[:]), in_=pw[:])
-            else:
-                nc.vector.tensor_copy(out=p_page[:].indirect(list1[:, 0:16]), in_=pw[:, 0:half])
-                nc.scalar.activation(out=p_page[:].indirect(list1[:, 16:32]), in_=pw[:, half:J], func=ACT.Copy)
-            adder = nc.gpsimd if t < PACK - 1 else nc.vector
-            adder.tensor_tensor(out=y[:, t, :], in0=p_page[:], in1=q_page[:], op=ALU.add)
+            pieces = 1 if t < PACK - 1 else 2
+            for h in range(pieces):
+                cols = slice(h * T // pieces, (h + 1) * T // pieces)
+                adder = nc.gpsimd if t < PACK - 1 else nc.vector
+                adder.tensor_tensor(out=y[:, t, cols], in0=p_page[:, cols], in1=q_page[:, cols], op=ALU.add)
             nc.sync.dma_start(out=out_rows[:, t, :], in_=y[:, t, :])
 
         y_codes = tile([P, T], U32, "y_codes")
         y_scale = tile([P, T], U8, "y_scale")
         words_out = out_1[0].rearrange("p c r -> p (c r)").bitcast(I32)
         width = T // 4
+        y_bf = [tile([P, width * PACK], BF16, f"y_bf{c}") for c in range(4)]
         for c in range(4):
             cols = slice(c * width, (c + 1) * width)
-            y_bf = tile([P, width * PACK], BF16, f"y_bf{c}")
-            dst = y_bf[:].rearrange("p (c i t) -> p c t i", i=4, t=PACK)
+            dst = y_bf[c][:].rearrange("p (c i t) -> p c t i", i=4, t=PACK)
             src = y[:, :, cols].rearrange("p t (c i) -> p c t i", i=4)
-            if c % 2 == 0:
+            if c % 2 == 1:
                 nc.vector.tensor_copy(out=dst, in_=src)
             else:
                 nc.scalar.copy(out=dst, in_=src)
-            nc.vector.quantize_mx(out=y_codes[:, cols].bitcast(FP8X4), scales=y_scale[:, cols], in_=y_bf[:])
-            if c % 2 == 1:
-                both = slice((c - 1) * width, (c + 1) * width)
-                nc.sync.dma_start(out=words_out[:, both], in_=y_codes[:, both].bitcast(I32))
+        for c in range(4):
+            cols = slice(c * width, (c + 1) * width)
+            nc.vector.quantize_mx(out=y_codes[:, cols].bitcast(FP8X4), scales=y_scale[:, cols], in_=y_bf[c][:])
+            if c > 0:
+                done = slice(0 if c == 1 else c * width, (c + 1) * width)
+                nc.sync.dma_start(out=words_out[:, done], in_=y_codes[:, done].bitcast(I32))
         for q in range(QUADS):
             nc.scalar.dma_start(out=out_2[0, 4 * q : 4 * q + 4, :].bitcast(I32), in_=y_scale[32 * q : 32 * q + 4, :].bitcast(I32))

@@ -1,4 +1,5 @@
 from contextlib import ExitStack
+from itertools import product
 
 import concourse.mybir as mybir
 
@@ -20,6 +21,10 @@ P = 128
 PACK = 4
 QUADS = 4
 PASSES = K // (P * PACK)
+LIST_COLS = J // 16
+SCALE_SPAN = 32 * (QUADS - 1) + 4
+PAGES = 2
+PLANE_CHUNKS = 4
 
 
 def tile_list_two_roads_one_layer_pl_kernel(tc, xq_words, xq_scales, wa, low_words, low_scales, up_words, up_scales, ga, offs, offs2, out_0, out_1, out_2):
@@ -28,180 +33,192 @@ def tile_list_two_roads_one_layer_pl_kernel(tc, xq_words, xq_scales, wa, low_wor
         keep = ctx.enter_context(tc.tile_pool(name="keep", bufs=1))
         psum = ctx.enter_context(tc.psum_pool(name="psum", bufs=1))
 
-        def tile(shape, dtype, name, tag=None):
-            return keep.tile(shape, dtype, name=name, tag=tag or name, align_bytes=64)
+        def tile(shape, dtype, name, after=None):
+            return keep.tile(shape, dtype, name=name, tag=after or name, align_bytes=64)
 
-        list1 = keep.tile([P, J // 16], U16, name="list1")
-        list2 = keep.tile([P, J // 16], U16, name="list2")
+        list1 = keep.tile([P, LIST_COLS], U16, name="list1")
+        list2 = keep.tile([P, LIST_COLS], U16, name="list2")
         x_words = [tile([P, T], U16, f"x_words{z}") for z in range(PASSES)]
         x_scales = tile([P, T], U8, "x_scales")
         low_raw = tile([P, PASSES, R], U32, "low_raw")
         low_scale_raw = tile([P, PASSES, R], U8, "low_scale_raw")
         up_raw = tile([P, N], U16, "up_raw")
-        up_scale_raw = tile([P, N], U8, "up_scale_raw")
-        wa_raw = [tile([P, PACK, N], F32, f"wa_raw{z}") for z in range(PASSES)]
-        gate = tile([P, J], F32, "gate")
         shifted = [tile([P, J], U8, f"shifted{a}") for a in range(2)]
-        p_pages = [tile([P, T], F32, f"p_page{a}") for a in range(2)]
-        q_pages = [tile([P, T], F32, f"q_page{a}") for a in range(2)]
+        q_pages = [tile([P, T], F32, f"q_page{a}") for a in range(PAGES)]
 
         nc.gpsimd.memset(x_scales[:].bitcast(I32), 0)
         nc.gpsimd.memset(low_scale_raw[:].rearrange("p z c -> p (z c)").bitcast(I32), 0)
-        for a in range(2):
-            nc.gpsimd.memset(shifted[1 - a][:].bitcast(I32), 0)
+        for plane in reversed(shifted):
+            nc.gpsimd.memset(plane[:].bitcast(I32), 0)
+        up_scale_raw = tile([P, N], U8, "up_scale_raw")
         nc.gpsimd.memset(up_scale_raw[:].bitcast(I32), 0)
-        for page in q_pages + p_pages:
+        for page in q_pages:
             nc.vector.memset(page[:], 0.0)
+        p_pages = [tile([P, T], F32, f"p_page{a}") for a in range(PAGES)]
+        for page in p_pages:
+            nc.gpsimd.memset(page[:], 0.0)
 
         wa_rows = wa.rearrange("(z p j) n -> z p j n", z=PASSES, j=PACK)
+        wa_raw = [tile([P, PACK, N], F32, "wa_raw0")]
         nc.sync.dma_start(list2[:], offs2)
         nc.sync.dma_start(out=x_words[0][:].bitcast(I32), in_=xq_words[0].bitcast(I32))
-        for q in range(QUADS):
-            nc.sync.dma_start(out=x_scales[32 * q : 32 * q + 8, :].bitcast(I32), in_=xq_scales[:, 4 * q : 4 * q + 4, :].bitcast(I32))
+        for g in range(QUADS):
+            nc.sync.dma_start(out=x_scales[32 * g : 32 * g + 8, :].bitcast(I32), in_=xq_scales[:, 4 * g : 4 * g + 4, :].bitcast(I32))
         nc.sync.dma_start(out=x_words[1][:].bitcast(I32), in_=xq_words[1].bitcast(I32))
         nc.sync.dma_start(out=low_raw[:].bitcast(I32), in_=low_words.rearrange("z p c r -> p z (c r)").bitcast(I32))
-        for q in range(QUADS):
-            nc.sync.dma_start(out=low_scale_raw[32 * q : 32 * q + 4, :, :].bitcast(I32), in_=low_scales[:, 4 * q : 4 * q + 4, :].rearrange("z r c -> r z c").bitcast(I32))
+        for g in range(QUADS):
+            nc.sync.dma_start(out=low_scale_raw[32 * g : 32 * g + 4, :, :].bitcast(I32), in_=low_scales[:, 4 * g : 4 * g + 4, :].rearrange("z r c -> r z c").bitcast(I32))
         nc.sync.dma_start(list1[:], offs)
-        for z in range(PASSES):
-            nc.sync.dma_start(out=wa_raw[z][:], in_=wa_rows[z])
+        nc.sync.dma_start(out=up_raw[:].bitcast(I32), in_=up_words[0].bitcast(I32))
+        nc.sync.dma_start(out=wa_raw[0][:], in_=wa_rows[0])
+        for g in range(QUADS):
+            nc.sync.dma_start(out=up_scale_raw[32 * g : 32 * g + 4, :].bitcast(I32), in_=up_scales[0, 4 * g : 4 * g + 4, :].bitcast(I32))
 
         def gather(offsets, a):
             words = [tile([P, J], U16, f"picked_words{a}{z}") for z in range(PASSES)]
             scales = tile([P, J], U8, f"picked_scales{a}")
+            nc.vector.tensor_copy(out=words[0][:], in_=x_words[0][:].indirect(offsets[:]))
             nc.vector.tensor_copy(out=scales[:], in_=x_scales[:].indirect(offsets[:]))
-            nc.sync.dma_start(out=shifted[a][0:100, :].bitcast(I32), in_=scales[4:104, :].bitcast(I32))
-            for z in range(PASSES):
-                nc.vector.tensor_copy(out=words[z][:], in_=x_words[z][:].indirect(offsets[:]))
+            nc.sync.dma_start(out=shifted[a][0:SCALE_SPAN, :].bitcast(I32), in_=scales[4 : 4 + SCALE_SPAN, :].bitcast(I32))
+            nc.vector.tensor_copy(out=words[1][:], in_=x_words[1][:].indirect(offsets[:]))
             return words, [scales, shifted[a]]
 
         words2, scales2 = gather(list2, 1)
-
-        nc.sync.dma_start(out=up_raw[:].bitcast(I32), in_=up_words[0].bitcast(I32))
-        for q in range(QUADS):
-            nc.sync.dma_start(out=up_scale_raw[32 * q : 32 * q + 4, :].bitcast(I32), in_=up_scales[0, 4 * q : 4 * q + 4, :].bitcast(I32))
-        nc.sync.dma_start(out=gate[:], in_=ga[0].partition_broadcast(P))
 
         low_codes = tile([P, PASSES, R], U32, "low_codes")
         low_scale = tile([P, PASSES, R], U8, "low_scale")
         nc.scalar.copy(out=low_codes[:].rearrange("p z (t m) -> p z m t", t=PACK), in_=low_raw[:].rearrange("p z (m t) -> p z m t", t=PACK))
         nc.vector.tensor_copy(out=low_scale[:].rearrange("p z (t m) -> p z t m", t=PACK), in_=low_scale_raw[:].rearrange("p z (m t) -> p z t m", t=PACK))
 
+        wa_raw.append(tile([P, PACK, N], F32, "wa_raw1", after="low_raw"))
+        nc.sync.dma_start(out=wa_raw[1][:], in_=wa_rows[1])
+
         words1, scales1 = gather(list1, 0)
 
+        gate = tile([P, J], F32, "gate", after="x_scales")
+        nc.sync.dma_start(out=gate[:], in_=ga[0].partition_broadcast(P))
+
         up_codes = tile([P, N], U16, "up_codes")
-        up_scale = tile([P, N], U8, "up_scale")
         wa_bf, wa_codes, wa_scale = {}, {}, {}
 
-        def round_wa(z, h, copy, tag=None):
-            wa_bf[z, h] = tile([P, 2 * P * PACK], BF16, f"wa_bf{z}{h}", tag)
-            copy(out=wa_bf[z, h][:].rearrange("p (e m j) -> p m j e", e=2, j=PACK), in_=wa_raw[z][:].rearrange("p j (m h e) -> p h m j e", h=2, e=2)[:, h])
+        def round_wa(z, h, after=None):
+            wa_bf[z, h] = tile([P, 2 * P * PACK], BF16, f"wa_bf{z}{h}", after)
+            nc.scalar.copy(out=wa_bf[z, h][:].rearrange("p (e m j) -> p m j e", e=2, j=PACK), in_=wa_raw[z][:].rearrange("p j (m h e) -> p h m j e", h=2, e=2)[:, h])
 
-        def quantise_wa(z, h, tag=None):
-            wa_codes[z, h] = tile([P, 2 * P], U32, f"wa_codes{z}{h}", tag)
+        def quantise_wa(z, h, after=None):
+            wa_codes[z, h] = tile([P, 2 * P], U32, f"wa_codes{z}{h}", after)
             wa_scale[z, h] = tile([P, 2 * P], U8, f"wa_scale{z}{h}")
             nc.vector.quantize_mx(out=wa_codes[z, h][:].bitcast(FP8X4), scales=wa_scale[z, h][:], in_=wa_bf[z, h][:])
 
         nc.scalar.copy(out=up_codes[:].rearrange("p (t m) -> p m t", t=PACK), in_=up_raw[:].rearrange("p (m t) -> p m t", t=PACK))
-        nc.vector.tensor_copy(out=up_scale[:].rearrange("p (t m) -> p t m", t=PACK), in_=up_scale_raw[:].rearrange("p (m t) -> p t m", t=PACK))
-        for h in range(2):
-            round_wa(0, h, nc.scalar.copy)
+        round_wa(0, 0)
+        wa_bf[0, 1] = tile([P, 2 * P * PACK], BF16, "wa_bf01")
+        nc.gpsimd.tensor_scalar(
+            out=wa_bf[0, 1][:].rearrange("p (e m j) -> p e m j", e=2, j=PACK),
+            in0=wa_raw[0][:].rearrange("p j (m h e) -> p h e m j", h=2, e=2)[:, 1],
+            scalar1=1.0,
+            scalar2=0.0,
+            op0=ALU.mult,
+            op1=ALU.add,
+        )
 
         v_bf = tile([P, J * PACK], BF16, "v_bf")
         v_codes = tile([P, J], U32, "v_codes")
         v_scale = tile([P, J], U8, "v_scale")
-        for c in range(J // P):
+        chunks = J // P
+        u_sums = [psum.tile([P, PACK, P], F32, name=f"u{c}", tag=f"second{c}") for c in range(chunks)]
+        for pair, z, member, t in product(range(chunks // 2), range(PASSES), range(2), range(PACK)):
+            c = 2 * pair + member
             cols = slice(c * P, (c + 1) * P)
-            u = psum.tile([P, PACK, P], F32, name="u", tag=f"second{c}")
-            for t in range(PACK):
-                for z in range(PASSES):
-                    nc.tensor.matmul_mx(
-                        out=u[:, t, :],
-                        lhsT=low_codes[:, z, t * P : (t + 1) * P].bitcast(FP8X4),
-                        lhsT_scale=low_scale[:, z, t * P : (t + 1) * P],
-                        rhs=words2[z][:, cols].bitcast(FP4X4),
-                        rhs_scale=scales2[z][:, cols],
-                        start=(z == 0),
-                        stop=(z == PASSES - 1),
-                    )
-            size = tile([P, P, PACK], F32, f"size{c}")
-            nc.scalar.activation(out=size[:], in_=u[:].rearrange("p t i -> p i t"), func=ACT.Abs)
+            nc.tensor.matmul_mx(
+                out=u_sums[c][:, t, :],
+                lhsT=low_codes[:, z, t * P : (t + 1) * P].bitcast(FP8X4),
+                lhsT_scale=low_scale[:, z, t * P : (t + 1) * P],
+                rhs=words2[z][:, cols].bitcast(FP4X4),
+                rhs_scale=scales2[z][:, cols],
+                start=(z == 0 and t == 0),
+                stop=(z == PASSES - 1 and t == PACK - 1),
+            )
+        for c in range(chunks):
+            u_by_token = u_sums[c][:].rearrange("p t i -> p i t")
+            u_abs = tile([P, P, PACK], F32, f"u_abs{c}")
+            nc.scalar.activation(out=u_abs[:], in_=u_by_token, func=ACT.Abs)
             nc.vector.scalar_tensor_tensor(
                 out=v_bf[:, c * P * PACK : (c + 1) * P * PACK].rearrange("p (i t) -> p i t", t=PACK),
-                in0=u[:].rearrange("p t i -> p i t"),
+                in0=u_by_token,
                 scalar=-0.5,
-                in1=size[:],
+                in1=u_abs[:],
                 op0=ALU.mult,
                 op1=ALU.add,
             )
-        quantise_wa(0, 0, "size3")
-        nc.vector.quantize_mx(out=v_codes[:].bitcast(FP8X4), scales=v_scale[:], in_=v_bf[:])
-        round_wa(1, 0, nc.scalar.copy, "size1")
+        up_scale = tile([P, N], U8, "up_scale", after="shifted1")
+        nc.vector.tensor_copy(out=up_scale[:].rearrange("p (t m) -> p t m", t=PACK), in_=up_scale_raw[:].rearrange("p (m t) -> p t m", t=PACK))
+        quantise_wa(0, 0, after="picked_words11")
+        round_wa(1, 0, after="low_scale")
         quantise_wa(1, 0)
-        round_wa(1, 1, nc.scalar.copy, "size2")
-        quantise_wa(0, 1, "v_bf")
+        nc.vector.quantize_mx(out=v_codes[:].bitcast(FP8X4), scales=v_scale[:], in_=v_bf[:])
+        round_wa(1, 1, after="low_codes")
+        quantise_wa(0, 1, after="low_scale")
         quantise_wa(1, 1)
 
         y = tile([P, PACK, T], F32, "y")
         out_rows = out_0.rearrange("(p t) c -> p t c", t=PACK)
-        half = J // 2
         for t in range(PACK):
-            rows = slice(t * P, (t + 1) * P)
-            q_sum = psum.tile([P, J], F32, name="q_sum", tag=f"second{t}")
-            nc.tensor.matmul_mx(
-                out=q_sum[:],
-                lhsT=up_codes[:, rows].bitcast(FP4X4),
-                lhsT_scale=up_scale[:, rows],
-                rhs=v_codes[:].bitcast(FP8X4),
-                rhs_scale=v_scale[:],
-                start=True,
-                stop=True,
-            )
-            p_sum = psum.tile([P, J], F32, name="p_sum", tag=f"first{t}")
+            p_sum = psum.tile([P, J], F32, name=f"p_sum{t}", tag="second0" if t == 1 else f"first{t}")
+            in_pair = slice((t % 2) * P, (t % 2 + 1) * P)
             for z in range(PASSES):
                 nc.tensor.matmul_mx(
                     out=p_sum[:],
-                    lhsT=wa_codes[z, t // 2][:, (t % 2) * P : (t % 2 + 1) * P].bitcast(FP8X4),
-                    lhsT_scale=wa_scale[z, t // 2][:, (t % 2) * P : (t % 2 + 1) * P],
+                    lhsT=wa_codes[z, t // 2][:, in_pair].bitcast(FP8X4),
+                    lhsT_scale=wa_scale[z, t // 2][:, in_pair],
                     rhs=words1[z][:].bitcast(FP4X4),
                     rhs_scale=scales1[z][:],
                     start=(z == 0),
                     stop=(z == PASSES - 1),
                 )
-            p_vals = tile([P, J], F32, f"p_vals{t}")
-            p_page = p_pages[t % len(p_pages)]
-            nc.vector.tensor_tensor(out=p_vals[:], in0=p_sum[:], in1=gate[:], op=ALU.mult)
-            nc.vector.tensor_copy(out=p_page[:].indirect(list1[:]), in_=p_vals[:])
-            q_vals = tile([P, J], F32, f"q_vals{t}")
+            q_sum = psum.tile([P, J], F32, name=f"q_sum{t}", tag=f"second{t}")
+            nc.tensor.matmul_mx(
+                out=q_sum[:],
+                lhsT=up_codes[:, t * P : (t + 1) * P].bitcast(FP4X4),
+                lhsT_scale=up_scale[:, t * P : (t + 1) * P],
+                rhs=v_codes[:].bitcast(FP8X4),
+                rhs_scale=v_scale[:],
+                start=True,
+                stop=True,
+            )
+            pw = tile([P, J], F32, f"pw{t}", after="low_codes" if t % 2 == 0 else "pw1")
+            p_page = p_pages[t % PAGES]
+            nc.vector.tensor_tensor(out=pw[:], in0=p_sum[:], in1=gate[:], op=ALU.mult)
+            nc.vector.tensor_copy(out=p_page[:].indirect(list1[:]), in_=pw[:])
+            q_vals = tile([P, J], F32, f"q_vals{t % 2}")
             nc.scalar.copy(out=q_vals[:], in_=q_sum[:])
-            q_page = q_pages[t % len(q_pages)]
-            for h in range(2):
-                nc.scalar.activation(out=q_page[:].indirect(list2[:, 16 * h : 16 * (h + 1)]), in_=q_vals[:, h * half : (h + 1) * half], func=ACT.Copy)
-            pieces = 1 if t < PACK - 1 else 2
-            for h in range(pieces):
-                cols = slice(h * T // pieces, (h + 1) * T // pieces)
-                adder = nc.gpsimd if t < PACK - 1 else nc.vector
-                adder.tensor_tensor(out=y[:, t, cols], in0=p_page[:, cols], in1=q_page[:, cols], op=ALU.add)
+            q_page = q_pages[t % PAGES]
+            for half in range(2):
+                entries = slice(half * J // 2, (half + 1) * J // 2)
+                nc.scalar.activation(out=q_page[:].indirect(list2[:, half * LIST_COLS // 2 : (half + 1) * LIST_COLS // 2]), in_=q_vals[:, entries], func=ACT.Copy)
+            if t < PACK - 1:
+                nc.gpsimd.tensor_tensor(out=y[:, t, :], in0=p_page[:], in1=q_page[:], op=ALU.add)
+            else:
+                for cols in (slice(0, T // 2), slice(T // 2, T)):
+                    nc.vector.tensor_tensor(out=y[:, t, cols], in0=p_page[:, cols], in1=q_page[:, cols], op=ALU.add)
             nc.sync.dma_start(out=out_rows[:, t, :], in_=y[:, t, :])
 
         y_codes = tile([P, T], U32, "y_codes")
         y_scale = tile([P, T], U8, "y_scale")
         words_out = out_1[0].rearrange("p c r -> p (c r)").bitcast(I32)
-        width = T // 4
-        y_bf = [tile([P, width * PACK], BF16, f"y_bf{c}") for c in range(4)]
-        for c in range(4):
-            cols = slice(c * width, (c + 1) * width)
-            dst = y_bf[c][:].rearrange("p (c i t) -> p c t i", i=4, t=PACK)
-            src = y[:, :, cols].rearrange("p t (c i) -> p c t i", i=4)
-            if c % 2 == 1:
-                nc.vector.tensor_copy(out=dst, in_=src)
-            else:
-                nc.scalar.copy(out=dst, in_=src)
-        for c in range(4):
+        width = T // PLANE_CHUNKS
+        y_bf = [tile([P, width * PACK], BF16, f"y_bf{c}") for c in range(PLANE_CHUNKS)]
+        for c in range(PLANE_CHUNKS):
+            copy = nc.scalar.copy if c % 2 == 0 else nc.vector.tensor_copy
+            copy(
+                out=y_bf[c][:].rearrange("p (c i t) -> p c t i", i=4, t=PACK),
+                in_=y[:, :, c * width : (c + 1) * width].rearrange("p t (c i) -> p c t i", i=4),
+            )
+        for c in range(PLANE_CHUNKS):
             cols = slice(c * width, (c + 1) * width)
             nc.vector.quantize_mx(out=y_codes[:, cols].bitcast(FP8X4), scales=y_scale[:, cols], in_=y_bf[c][:])
             if c > 0:
                 done = slice(0 if c == 1 else c * width, (c + 1) * width)
                 nc.sync.dma_start(out=words_out[:, done], in_=y_codes[:, done].bitcast(I32))
-        for q in range(QUADS):
-            nc.scalar.dma_start(out=out_2[0, 4 * q : 4 * q + 4, :].bitcast(I32), in_=y_scale[32 * q : 32 * q + 4, :].bitcast(I32))
+        for g in range(QUADS):
+            nc.scalar.dma_start(out=out_2[0, 4 * g : 4 * g + 4, :].bitcast(I32), in_=y_scale[32 * g : 32 * g + 4, :].bitcast(I32))

from contextlib import ExitStack
from itertools import product

import concourse.mybir as mybir

K, T, J, N, R = 1024, 1024, 512, 512, 512
FLOPS = 2 * K * N * J + 2 * K * R * J + 2 * R * N * J

F32 = mybir.dt.float32
BF16 = mybir.dt.bfloat16
I32 = mybir.dt.int32
U32 = mybir.dt.uint32
U16 = mybir.dt.uint16
U8 = mybir.dt.uint8
FP8X4 = mybir.dt.float8_e4m3fn_x4
FP4X4 = mybir.dt.float4_e2m1fn_x4
ALU = mybir.AluOpType
ACT = mybir.ActivationFunctionType

P = 128
PACK = 4
QUADS = 4
PASSES = K // (P * PACK)
LIST_COLS = J // 16
SCALE_SPAN = 32 * (QUADS - 1) + 4
PAGES = 2
PLANE_CHUNKS = 4


def tile_list_two_roads_one_layer_pl_kernel(tc, xq_words, xq_scales, wa, low_words, low_scales, up_words, up_scales, ga, offs, offs2, out_0, out_1, out_2):
    nc = tc.nc
    with ExitStack() as ctx:
        keep = ctx.enter_context(tc.tile_pool(name="keep", bufs=1))
        psum = ctx.enter_context(tc.psum_pool(name="psum", bufs=1))

        def tile(shape, dtype, name, after=None):
            return keep.tile(shape, dtype, name=name, tag=after or name, align_bytes=64)

        list1 = keep.tile([P, LIST_COLS], U16, name="list1")
        list2 = keep.tile([P, LIST_COLS], U16, name="list2")
        x_words = [tile([P, T], U16, f"x_words{z}") for z in range(PASSES)]
        x_scales = tile([P, T], U8, "x_scales")
        low_raw = tile([P, PASSES, R], U32, "low_raw")
        low_scale_raw = tile([P, PASSES, R], U8, "low_scale_raw")
        up_raw = tile([P, N], U16, "up_raw")
        shifted = [tile([P, J], U8, f"shifted{a}") for a in range(2)]
        q_pages = [tile([P, T], F32, f"q_page{a}") for a in range(PAGES)]

        nc.gpsimd.memset(x_scales[:].bitcast(I32), 0)
        nc.gpsimd.memset(low_scale_raw[:].rearrange("p z c -> p (z c)").bitcast(I32), 0)
        for plane in reversed(shifted):
            nc.gpsimd.memset(plane[:].bitcast(I32), 0)
        up_scale_raw = tile([P, N], U8, "up_scale_raw")
        nc.gpsimd.memset(up_scale_raw[:].bitcast(I32), 0)
        for page in q_pages:
            nc.vector.memset(page[:], 0.0)
        p_pages = [tile([P, T], F32, f"p_page{a}") for a in range(PAGES)]
        for page in p_pages:
            nc.gpsimd.memset(page[:], 0.0)

        wa_rows = wa.rearrange("(z p j) n -> z p j n", z=PASSES, j=PACK)
        wa_raw = [tile([P, PACK, N], F32, "wa_raw0")]
        nc.sync.dma_start(list2[:], offs2)
        nc.sync.dma_start(out=x_words[0][:].bitcast(I32), in_=xq_words[0].bitcast(I32))
        for g in range(QUADS):
            nc.sync.dma_start(out=x_scales[32 * g : 32 * g + 8, :].bitcast(I32), in_=xq_scales[:, 4 * g : 4 * g + 4, :].bitcast(I32))
        nc.sync.dma_start(out=x_words[1][:].bitcast(I32), in_=xq_words[1].bitcast(I32))
        nc.sync.dma_start(out=low_raw[:].bitcast(I32), in_=low_words.rearrange("z p c r -> p z (c r)").bitcast(I32))
        for g in range(QUADS):
            nc.sync.dma_start(out=low_scale_raw[32 * g : 32 * g + 4, :, :].bitcast(I32), in_=low_scales[:, 4 * g : 4 * g + 4, :].rearrange("z r c -> r z c").bitcast(I32))
        nc.sync.dma_start(list1[:], offs)
        nc.sync.dma_start(out=up_raw[:].bitcast(I32), in_=up_words[0].bitcast(I32))
        nc.sync.dma_start(out=wa_raw[0][:], in_=wa_rows[0])
        for g in range(QUADS):
            nc.sync.dma_start(out=up_scale_raw[32 * g : 32 * g + 4, :].bitcast(I32), in_=up_scales[0, 4 * g : 4 * g + 4, :].bitcast(I32))

        def gather(offsets, a):
            words = [tile([P, J], U16, f"picked_words{a}{z}") for z in range(PASSES)]
            scales = tile([P, J], U8, f"picked_scales{a}")
            nc.vector.tensor_copy(out=words[0][:], in_=x_words[0][:].indirect(offsets[:]))
            nc.vector.tensor_copy(out=scales[:], in_=x_scales[:].indirect(offsets[:]))
            nc.sync.dma_start(out=shifted[a][0:SCALE_SPAN, :].bitcast(I32), in_=scales[4 : 4 + SCALE_SPAN, :].bitcast(I32))
            nc.vector.tensor_copy(out=words[1][:], in_=x_words[1][:].indirect(offsets[:]))
            return words, [scales, shifted[a]]

        words2, scales2 = gather(list2, 1)

        low_codes = tile([P, PASSES, R], U32, "low_codes")
        low_scale = tile([P, PASSES, R], U8, "low_scale")
        nc.scalar.copy(out=low_codes[:].rearrange("p z (t m) -> p z m t", t=PACK), in_=low_raw[:].rearrange("p z (m t) -> p z m t", t=PACK))
        nc.vector.tensor_copy(out=low_scale[:].rearrange("p z (t m) -> p z t m", t=PACK), in_=low_scale_raw[:].rearrange("p z (m t) -> p z t m", t=PACK))

        wa_raw.append(tile([P, PACK, N], F32, "wa_raw1", after="low_raw"))
        nc.sync.dma_start(out=wa_raw[1][:], in_=wa_rows[1])

        words1, scales1 = gather(list1, 0)

        gate = tile([P, J], F32, "gate", after="x_scales")
        nc.sync.dma_start(out=gate[:], in_=ga[0].partition_broadcast(P))

        up_codes = tile([P, N], U16, "up_codes")
        wa_bf, wa_codes, wa_scale = {}, {}, {}

        def round_wa(z, h, after=None):
            wa_bf[z, h] = tile([P, 2 * P * PACK], BF16, f"wa_bf{z}{h}", after)
            nc.scalar.copy(out=wa_bf[z, h][:].rearrange("p (e m j) -> p m j e", e=2, j=PACK), in_=wa_raw[z][:].rearrange("p j (m h e) -> p h m j e", h=2, e=2)[:, h])

        def quantise_wa(z, h, after=None):
            wa_codes[z, h] = tile([P, 2 * P], U32, f"wa_codes{z}{h}", after)
            wa_scale[z, h] = tile([P, 2 * P], U8, f"wa_scale{z}{h}")
            nc.vector.quantize_mx(out=wa_codes[z, h][:].bitcast(FP8X4), scales=wa_scale[z, h][:], in_=wa_bf[z, h][:])

        nc.scalar.copy(out=up_codes[:].rearrange("p (t m) -> p m t", t=PACK), in_=up_raw[:].rearrange("p (m t) -> p m t", t=PACK))
        round_wa(0, 0)
        wa_bf[0, 1] = tile([P, 2 * P * PACK], BF16, "wa_bf01")
        nc.gpsimd.tensor_scalar(
            out=wa_bf[0, 1][:].rearrange("p (e m j) -> p e m j", e=2, j=PACK),
            in0=wa_raw[0][:].rearrange("p j (m h e) -> p h e m j", h=2, e=2)[:, 1],
            scalar1=1.0,
            scalar2=0.0,
            op0=ALU.mult,
            op1=ALU.add,
        )

        v_bf = tile([P, J * PACK], BF16, "v_bf")
        v_codes = tile([P, J], U32, "v_codes")
        v_scale = tile([P, J], U8, "v_scale")
        chunks = J // P
        u_sums = [psum.tile([P, PACK, P], F32, name=f"u{c}", tag=f"second{c}") for c in range(chunks)]
        for pair, z, member, t in product(range(chunks // 2), range(PASSES), range(2), range(PACK)):
            c = 2 * pair + member
            cols = slice(c * P, (c + 1) * P)
            nc.tensor.matmul_mx(
                out=u_sums[c][:, t, :],
                lhsT=low_codes[:, z, t * P : (t + 1) * P].bitcast(FP8X4),
                lhsT_scale=low_scale[:, z, t * P : (t + 1) * P],
                rhs=words2[z][:, cols].bitcast(FP4X4),
                rhs_scale=scales2[z][:, cols],
                start=(z == 0 and t == 0),
                stop=(z == PASSES - 1 and t == PACK - 1),
            )
        for c in range(chunks):
            u_by_token = u_sums[c][:].rearrange("p t i -> p i t")
            u_abs = tile([P, P, PACK], F32, f"u_abs{c}")
            nc.scalar.activation(out=u_abs[:], in_=u_by_token, func=ACT.Abs)
            nc.vector.scalar_tensor_tensor(
                out=v_bf[:, c * P * PACK : (c + 1) * P * PACK].rearrange("p (i t) -> p i t", t=PACK),
                in0=u_by_token,
                scalar=-0.5,
                in1=u_abs[:],
                op0=ALU.mult,
                op1=ALU.add,
            )
        up_scale = tile([P, N], U8, "up_scale", after="shifted1")
        nc.vector.tensor_copy(out=up_scale[:].rearrange("p (t m) -> p t m", t=PACK), in_=up_scale_raw[:].rearrange("p (m t) -> p t m", t=PACK))
        quantise_wa(0, 0, after="picked_words11")
        round_wa(1, 0, after="low_scale")
        quantise_wa(1, 0)
        nc.vector.quantize_mx(out=v_codes[:].bitcast(FP8X4), scales=v_scale[:], in_=v_bf[:])
        round_wa(1, 1, after="low_codes")
        quantise_wa(0, 1, after="low_scale")
        quantise_wa(1, 1)

        y = tile([P, PACK, T], F32, "y")
        out_rows = out_0.rearrange("(p t) c -> p t c", t=PACK)
        for t in range(PACK):
            p_sum = psum.tile([P, J], F32, name=f"p_sum{t}", tag="second0" if t == 1 else f"first{t}")
            in_pair = slice((t % 2) * P, (t % 2 + 1) * P)
            for z in range(PASSES):
                nc.tensor.matmul_mx(
                    out=p_sum[:],
                    lhsT=wa_codes[z, t // 2][:, in_pair].bitcast(FP8X4),
                    lhsT_scale=wa_scale[z, t // 2][:, in_pair],
                    rhs=words1[z][:].bitcast(FP4X4),
                    rhs_scale=scales1[z][:],
                    start=(z == 0),
                    stop=(z == PASSES - 1),
                )
            q_sum = psum.tile([P, J], F32, name=f"q_sum{t}", tag=f"second{t}")
            nc.tensor.matmul_mx(
                out=q_sum[:],
                lhsT=up_codes[:, t * P : (t + 1) * P].bitcast(FP4X4),
                lhsT_scale=up_scale[:, t * P : (t + 1) * P],
                rhs=v_codes[:].bitcast(FP8X4),
                rhs_scale=v_scale[:],
                start=True,
                stop=True,
            )
            pw = tile([P, J], F32, f"pw{t}", after="low_codes" if t % 2 == 0 else "pw1")
            p_page = p_pages[t % PAGES]
            nc.vector.tensor_tensor(out=pw[:], in0=p_sum[:], in1=gate[:], op=ALU.mult)
            nc.vector.tensor_copy(out=p_page[:].indirect(list1[:]), in_=pw[:])
            q_vals = tile([P, J], F32, f"q_vals{t % 2}")
            nc.scalar.copy(out=q_vals[:], in_=q_sum[:])
            q_page = q_pages[t % PAGES]
            for half in range(2):
                entries = slice(half * J // 2, (half + 1) * J // 2)
                nc.scalar.activation(out=q_page[:].indirect(list2[:, half * LIST_COLS // 2 : (half + 1) * LIST_COLS // 2]), in_=q_vals[:, entries], func=ACT.Copy)
            if t < PACK - 1:
                nc.gpsimd.tensor_tensor(out=y[:, t, :], in0=p_page[:], in1=q_page[:], op=ALU.add)
            else:
                for cols in (slice(0, T // 2), slice(T // 2, T)):
                    nc.vector.tensor_tensor(out=y[:, t, cols], in0=p_page[:, cols], in1=q_page[:, cols], op=ALU.add)
            nc.sync.dma_start(out=out_rows[:, t, :], in_=y[:, t, :])

        y_codes = tile([P, T], U32, "y_codes")
        y_scale = tile([P, T], U8, "y_scale")
        words_out = out_1[0].rearrange("p c r -> p (c r)").bitcast(I32)
        width = T // PLANE_CHUNKS
        y_bf = [tile([P, width * PACK], BF16, f"y_bf{c}") for c in range(PLANE_CHUNKS)]
        for c in range(PLANE_CHUNKS):
            copy = nc.scalar.copy if c % 2 == 0 else nc.vector.tensor_copy
            copy(
                out=y_bf[c][:].rearrange("p (c i t) -> p c t i", i=4, t=PACK),
                in_=y[:, :, c * width : (c + 1) * width].rearrange("p t (c i) -> p c t i", i=4),
            )
        for c in range(PLANE_CHUNKS):
            cols = slice(c * width, (c + 1) * width)
            nc.vector.quantize_mx(out=y_codes[:, cols].bitcast(FP8X4), scales=y_scale[:, cols], in_=y_bf[c][:])
            if c > 0:
                done = slice(0 if c == 1 else c * width, (c + 1) * width)
                nc.sync.dma_start(out=words_out[:, done], in_=y_codes[:, done].bitcast(I32))
        for g in range(QUADS):
            nc.scalar.dma_start(out=out_2[0, 4 * g : 4 * g + 4, :].bitcast(I32), in_=y_scale[32 * g : 32 * g + 4, :].bitcast(I32))
